import numpy as np
CORES = [24,40,56,80,88,96]
N = 6
C = 512
def setup_inputs(rng):
    return {"x": rng.standard_normal((N, 128, C), dtype=np.float32)}
def setup_inputs_big(rng):
    d = setup_inputs(rng)
    for k in ("x",): d[k] = (d[k].astype(np.float32) * 1048576.0).astype(d[k].dtype)
    return d
def setup_inputs_small(rng):
    d = setup_inputs(rng)
    for k in ("x",): d[k] = (d[k].astype(np.float32) * (1 / 1048576.0)).astype(d[k].dtype)
    return d
def setup_inputs_apart(rng):
    d = setup_inputs(rng)
    f = (10.0 ** rng.permutation(np.linspace(-1.5, 1.5, N))).astype(np.float32).reshape(N, 1, 1)
    for k in ("x",): d[k] = (d[k].astype(np.float32) * f).astype(d[k].dtype)
    return d
def reference(x):
    X = x.astype(np.float64)
    y = np.stack([sum(np.maximum(X[r] - X[s], 0.0) for s in range(N)) for r in range(N)])
    return {"y": y.astype(np.float32)}

from concourse.bass import DstId, RemoteDMATransfer
from concourse.mybir import AluOpType

N = 6
C = 512
NDIRECT = 2

SCRATCH = {
    "xs": ("sbuf", [128, C], "float32"),
    "xin": ("sbuf", [128, N * C], "float32"),
    "hb": ("sbuf", [128, C], "float32"),
    "m": ("sbuf", [128, N * C], "float32"),
    "five": ("sbuf", [128, C], "float32"),
    "ys": ("sbuf", [128, C], "float32"),
    "xr": ("psum", [128, C], "float32"),
    "acc": ("psum", [128, C], "float32"),
}
SEMAPHORES = ["ld", "fed", "sent", "v", "st"] + ["arr%d" % s for s in range(N)]


def _bits(mask):
    return [b for b in range(mask.bit_length()) if (mask >> b) & 1]


def _mask_of(bits):
    m = 0
    for b in bits:
        m |= 1 << b
    return m


def _plan(T, topo):
    ranks = list(T.cores)
    n = len(ranks)
    every = range(topo.CHIPS * topo.CORES_PER_CHIP)
    helpers, direct, relayed = [], [], []
    for s in range(n):
        me = ranks[s]
        helpers.append([c for c in every if topo.chip(c) == topo.chip(me) and c != me
                        and all(topo.may_write(c, d) for d in ranks)])
        same = [r for r in range(n) if r != s and topo.may_write(me, ranks[r])]
        cross = [r for r in range(n) if r != s and r not in same]
        grp = sorted(same + [s])
        i = grp.index(s)
        cyc = [grp[(i + k) % len(grp)] for k in range(1, len(grp))]
        rot = (i * len(cross)) // len(grp) if cross else 0
        direct.append(cyc[:NDIRECT])
        relayed.append(cross[rot:] + cross[:rot] + cyc[NDIRECT:])
    order = []
    for r in range(n):
        exp = []
        for s in range(n):
            if r in direct[s]:
                exp.append((3.9 + 2.1 * (direct[s].index(r) + 1), s))
            elif r in relayed[s]:
                exp.append((5.8 + 0.9 * (relayed[s].index(r) + 1), s))
        order.append([s for _, s in sorted(exp)])
    return ranks, helpers, direct, relayed, order


def _send(g, T, topo, core, dst, out_ap, in_ap, sem):
    rid, pid, _ = topo.addr(dst)
    mask = topo.mask(core, dst)
    g.remote_dma(out_ap, in_ap, sem, T.sem.sent, pid, rid, mask)
    return len(_bits(mask))


def rank_program(g, core, T, topo):
    ranks, helpers, direct, relayed, order = _plan(T, topo)
    rank = T.rank_of(core)

    if rank is None:
        for s in range(len(ranks)):
            if core in helpers[s]:
                nh = len(helpers[s])
                w = C // nh
                q = helpers[s].index(core)
                fed = len(_bits(topo.mask(ranks[s], core))) // nh
                g.wait_ge(T.sem.fed, fed)
                sent = 0
                for r in relayed[s]:
                    sent += _send(g, T, topo, core, ranks[r], T.xin[:, s * C + q * w: s * C + (q + 1) * w],
                                  T.hb[:, 0:w], T.sem["arr%d" % s])
                g.wait_ge(T.sem.sent, sent)
        return

    s = rank
    hs = helpers[s]
    nh = len(hs)
    w = C // nh
    g.sync.dma_start(T.xs[:, :], T.x[:, :]).then_inc(T.sem.ld, 16)

    g.wait_ge(T.sem.ld, 16)
    trs = []
    sent = 0
    for q, h in enumerate(hs):
        rid, pid, _ = topo.addr(h)
        bits = _bits(topo.mask(core, h))
        per = len(bits) // nh
        trs.append(RemoteDMATransfer(dst_ids=[DstId(rid=rid, pnc=pid)], dma_engine_mask=_mask_of(bits[q * per:(q + 1) * per]),
                                     remote_sem=T.sem.fed, src=T.xs[:, q * w:(q + 1) * w], dst=T.hb[:, 0:w]))
        sent += per
    g.remote_dma_fused(trs, local_sem=T.sem.sent)
    for r in direct[s]:
        sent += _send(g, T, topo, core, ranks[r], T.xin[:, s * C:(s + 1) * C], T.xs[:, :], T.sem["arr%d" % s])

    v = g.vector
    nv = 0
    v.memset(T.five[:, :], 5.0).then_inc(T.sem.v, 1)
    nv += 1
    v.wait_ge(T.sem.ld, 16)
    v.tensor_copy(T.xr[:, :], T.xs[:, :]).then_inc(T.sem.v, 1)
    nv += 1
    v.wait_ge(T.sem.v, 1)
    v.tensor_tensor(T.acc[:, :], T.xs[:, :], T.five[:, :], AluOpType.mult).then_inc(T.sem.v, 1)
    nv += 1
    for k, src in enumerate(order[s]):
        if s in direct[src]:
            need = len(_bits(topo.mask(ranks[src], core)))
        else:
            need = sum(len(_bits(topo.mask(h, core))) for h in helpers[src])
        v.wait_ge(T.sem["arr%d" % src], need)
        v.wait_ge(T.sem.v, nv)
        mk = T.m[:, k * C:(k + 1) * C]
        v.tensor_tensor(mk, T.xr[:, :], T.xin[:, src * C:(src + 1) * C], AluOpType.min).then_inc(T.sem.v, 1)
        nv += 1
        v.wait_ge(T.sem.v, nv)
        out = T.ys[:, :] if k == len(order[s]) - 1 else T.acc[:, :]
        v.tensor_tensor(out, T.acc[:, :], mk, AluOpType.subtract).then_inc(T.sem.v, 1)
        nv += 1

    g.sync.wait_ge(T.sem.v, nv)
    g.sync.dma_start(T.y[:, :], T.ys[:, :]).then_inc(T.sem.st, 16)
    g.sync.wait_ge(T.sem.st, 16)
    g.wait_ge(T.sem.sent, sent)
